import numpy as np
import ml_dtypes


def mxq(x, axis, fmt="e4m3"):
    dtype, down = {"e4m3": (ml_dtypes.float8_e4m3fn, 7), "e5m2": (ml_dtypes.float8_e5m2, 14)}[fmt]
    v = np.moveaxis(np.asarray(x, np.float32).astype(ml_dtypes.bfloat16).astype(np.float64), axis, -1)
    blocks = v.reshape(v.shape[:-1] + (-1, 32))
    amax = np.abs(blocks).max(-1, keepdims=True)
    byte = np.maximum(np.where(amax > 0, np.frexp(amax)[1] - 1 + 127, 0) - down, 1)
    scale = np.exp2(byte - 127.0)
    codes = (blocks / scale).astype(np.float32).astype(dtype).astype(np.float64)
    return np.moveaxis((codes * scale).reshape(v.shape), -1, axis)


WIDE = False


def mx_kscale(k):
    if not WIDE:
        return np.ones(k)
    levels = np.array([10, -10, 5, -5, 0])
    if k % 512:
        return np.exp2(np.random.permutation(np.resize(levels, k // 32))).repeat(32)
    a = np.empty((k // 512, 16))
    for p in range(k // 512):
        a[p, :8] = np.random.permutation(np.resize(levels, 8))
        for g in range(8):
            far = levels[np.abs(levels - a[p, g]) >= 10]
            a[p, g + 8] = far[np.random.randint(len(far))]
    return np.exp2(a.ravel()).repeat(32)


def f64(x):
    return np.asarray(x).astype(np.float64)


def striped(idx):
    return np.tile(idx.reshape(-1, 16).T, (8, 1)).astype(np.uint16)


def unstriped(offs):
    return offs[:16].T.reshape(-1).astype(np.int64)


E2M1 = np.array([0.0, 0.5, 1.0, 1.5, 2.0, 3.0, 4.0, 6.0, -0.0, -0.5, -1.0, -1.5, -2.0, -3.0, -4.0, -6.0])


def pack_weight(w, fmt):
    k, n = w.shape
    w = f64(np.asarray(w, np.float32).astype(ml_dtypes.bfloat16)).reshape(k // 32, 32, n)
    amax = np.abs(w).max(1)
    if fmt == "e4m3":
        byte = np.frexp(amax)[1] - 1 + 127 - 7
    else:
        mant, ex = np.frexp(amax / 6.0)
        byte = np.where(mant > 0.5, ex, ex - 1) + 127
    byte = np.clip(np.where(amax > 0, byte, 1), 1, 254)
    scaled = (w * np.exp2(127.0 - byte)[:, None, :]).reshape(k, n).astype(np.float32)
    by_word = np.ascontiguousarray(scaled.reshape(k // 512, 128, 4, n).transpose(0, 1, 3, 2))
    if fmt == "e4m3":
        words = by_word.astype(ml_dtypes.float8_e4m3fn).view(np.uint8)
    else:
        c = by_word.astype(ml_dtypes.float4_e2m1fn).view(np.uint8) & 0xF
        words = (c[..., 0::2] | (c[..., 1::2] << 4)).reshape(k // 512, 128, 2 * n)
    return np.ascontiguousarray(words), np.ascontiguousarray(byte.astype(np.uint8).reshape(k // 512, 16, n))


def unpack_weight(words, scales, fmt):
    g, _, n = scales.shape
    words = np.ascontiguousarray(words).reshape(g, 128, n, -1)
    if fmt == "e4m3":
        vals = words.view(ml_dtypes.float8_e4m3fn).astype(np.float64)
    else:
        nib = np.empty((g, 128, n, 4), np.uint8)
        nib[..., 0::2] = words & 0xF
        nib[..., 1::2] = words >> 4
        vals = E2M1[nib]
    vals = vals * np.repeat(np.exp2(scales.astype(np.float64) - 127.0), 8, axis=1)[..., None]
    return vals.transpose(0, 1, 3, 2).reshape(g * 512, n)


def gelu(v):
    return 0.5 * v * (1.0 + np.tanh(np.sqrt(2.0 / np.pi) * (v + 0.044715 * v**3)))


def striped8(idx):
    return np.concatenate([v.reshape(-1, 16).T for v in idx]).astype(np.uint16)


def unstriped8(offs):
    return np.stack([offs[16 * g:16 * g + 16].T.reshape(-1) for g in range(8)]).astype(np.int64)


def put_heads(h, wgs, idx8, t2):
    r = np.arange(h.shape[0])
    page = np.zeros((h.shape[0], t2))
    page[r[:, None], idx8[r % 512 // 64]] = wgs[r // 4 % 128] * h
    return page


K, T, S, T2, H, N = 1536, 2048, 512, 1024, 1024, 384

def setup_inputs():
    n = np.random.standard_normal
    s = mx_kscale(K)[:, None]
    u = mx_kscale(H)[:, None]
    tab_words, tab_scales = pack_weight(n((K, T)) * s, "e4m3")
    wd_words, wd_scales = pack_weight(n((H, N)) / np.sqrt(H) / u, "e2m1")
    return {
        "tab_words": tab_words, "tab_scales": tab_scales,
        "offs": striped(np.random.permutation(T)[:S]),
        "w1": (n((K, H)) / np.sqrt(K) / s * u.T).astype(np.float32),
        "offs2": striped8(np.stack([np.random.permutation(T2)[:S] for _ in range(8)])),
        "wgs": np.repeat(np.random.uniform(0.5, 2.0, (8, S)), 16, axis=0).astype(np.float32),
        "inv": (n((H, T2)) * u).astype(np.float32),
        "wd_words": wd_words, "wd_scales": wd_scales,
        "wc": (n((H, N)) / np.sqrt(H) / u).astype(np.float32),
    }

def reference(tab_words, tab_scales, offs, w1, offs2, wgs, inv, wd_words, wd_scales, wc):
    v = unpack_weight(tab_words, tab_scales, "e4m3")[:, unstriped(offs)]
    h = mxq(f64(w1), 0, "e4m3").T @ v
    page = put_heads(h, f64(wgs), unstriped8(offs2), T2)
    z = page + f64(inv)
    dis = mxq(np.maximum(z, 0.0), 0, "e4m3")
    chg = mxq(np.minimum(z, 0.0), 0, "e4m3")
    wd = unpack_weight(wd_words, wd_scales, "e2m1")
    out = wd.T @ dis + mxq(f64(wc), 0, "e4m3").T @ chg
    return out

@@ -1,0 +1,268 @@
+from contextlib import ExitStack
+
+import concourse.mybir as mybir
+
+K, T, S, T2, H, N = 1536, 2048, 512, 1024, 1024, 384
+FLOPS = 2 * K * H * S + 4 * H * N * T2
+
+F32 = mybir.dt.float32
+BF16 = mybir.dt.bfloat16
+I32 = mybir.dt.int32
+U32 = mybir.dt.uint32
+U16 = mybir.dt.uint16
+U8 = mybir.dt.uint8
+FP8X4 = mybir.dt.float8_e4m3fn_x4
+FP4X4 = mybir.dt.float4_e2m1fn_x4
+ALU = mybir.AluOpType
+ACT = mybir.ActivationFunctionType
+
+P = 128
+PACK = 4
+PASS = P * PACK
+KP = K // PASS
+RP = H // PASS
+HALF = 512
+NT = N // P
+
+
+def tile_list_battery_dispatch_split_kernel(
+    tc, tab_words, tab_scales, offs, w1, offs2, wgs, inv, wd_words, wd_scales, wc, out
+):
+    nc = tc.nc
+    with ExitStack() as ctx:
+        keep = ctx.enter_context(tc.tile_pool(name="keep", bufs=1))
+        ring = ctx.enter_context(tc.tile_pool(name="ring", bufs=3))
+        ring4 = ctx.enter_context(tc.tile_pool(name="ring4", bufs=4))
+        hps = ctx.enter_context(tc.psum_pool(name="hps", bufs=2))
+        ops = ctx.enter_context(tc.psum_pool(name="ops", bufs=1))
+
+        list1 = keep.tile([P, S // 16], U16, name="list1")
+        list2 = keep.tile([P, S // 16], U16, name="list2")
+        tab = [keep.tile([P, T], U32, name=f"tab{a}") for a in range(KP)]
+        tab_sc = keep.tile([P, T], U8, name="tab_sc", align_bytes=64)
+        wd_sc = keep.tile([P, RP * N], U8, name="wd_sc", align_bytes=64)
+        wd_w = keep.tile([P, RP * 2 * N], U8, name="wd_w", align_bytes=64)
+        wgs_sb = keep.tile([P, S], F32, name="wgs_sb")
+        pages = [keep.tile([P, T2], F32, name=f"page{i}") for i in range(PACK)]
+
+        nc.vector.memset(tab_sc[:].bitcast(I32), 0)
+        nc.vector.memset(wd_sc[:].bitcast(I32), 0)
+        for page in pages:
+            nc.vector.memset(page[:], 0.0)
+
+        def load_w1(a, c0, width):
+            raw = keep.tile([P, PACK, width], F32, name=f"w1raw{a}_{c0}")
+            rows = w1[a * PASS : (a + 1) * PASS, c0 : c0 + width]
+            nc.sync.dma_start(out=raw[:], in_=rows.rearrange("(p j) c -> p j c", j=PACK))
+            return raw
+
+        def load_tab(a):
+            nc.sync.dma_start(
+                out=tab[a][:].bitcast(I32), in_=tab_words[a].rearrange("p t i -> p (t i)").bitcast(I32)
+            )
+
+        nc.sync.dma_start(list1[:], offs)
+        load_tab(0)
+        for q in range(4):
+            nc.scalar.dma_start(
+                out=tab_sc[32 * q : 32 * q + 4 * KP, :].bitcast(I32),
+                in_=tab_scales[:, 4 * q : 4 * q + 4, :].bitcast(I32),
+            )
+        w1raw = {}
+        w1raw[0, 0] = [load_w1(0, 0, PASS)]
+        load_tab(1)
+        w1raw[0, 1] = [load_w1(1, 0, PASS)]
+        nc.sync.dma_start(list2[:], offs2)
+        nc.sync.dma_start(out=wgs_sb[:], in_=wgs)
+        load_tab(2)
+        w1raw[0, 2] = [load_w1(2, 0, PASS // 2), load_w1(2, PASS // 2, PASS // 2)]
+        for a in range(KP):
+            w1raw[1, a] = [load_w1(a, PASS, PASS)]
+
+        inv_sb = {}
+
+        def load_inv(b):
+            rows = inv[b * PASS : (b + 1) * PASS, :].rearrange("(p j) m -> p j m", j=PACK)
+            for i in range(PACK):
+                inv_sb[b, i] = keep.tile([P, T2], F32, name=f"inv{b}_{i}")
+                nc.sync.dma_start(out=inv_sb[b, i][:], in_=rows[:, i, :])
+
+        load_inv(0)
+        wcraw = []
+        for b in range(RP):
+            wcraw.append(keep.tile([P, PACK, N], F32, name=f"wcraw{b}"))
+            nc.sync.dma_start(
+                out=wcraw[b][:], in_=wc[b * PASS : (b + 1) * PASS, :].rearrange("(p j) n -> p j n", j=PACK)
+            )
+        nc.sync.dma_start(
+            out=wd_w[:].bitcast(I32).rearrange("p (b c) -> p b c", b=RP),
+            in_=wd_words.bitcast(I32).rearrange("b p c -> p b c"),
+        )
+        for q in range(4):
+            nc.sync.dma_start(
+                out=wd_sc[32 * q : 32 * q + 4, :].bitcast(I32).rearrange("r (b c) -> r b c", b=RP),
+                in_=wd_scales[:, 4 * q : 4 * q + 4, :].bitcast(I32).rearrange("b r c -> r b c"),
+            )
+        load_inv(1)
+
+        v_sc = keep.tile([P, S], U8, name="v_sc", align_bytes=64)
+        v_w = [keep.tile([P, S], U32, name=f"v_w{a}", align_bytes=64) for a in range(KP)]
+        nc.vector.tensor_copy(v_w[0][:], tab[0][:].indirect(list1[:]))
+        nc.vector.tensor_copy(v_sc[:], tab_sc[:].indirect(list1[:]))
+
+        w1_w = {}
+        w1_sc = {}
+
+        def quant_w1(b, a):
+            grouped = ring.tile([P, PACK * PASS], BF16, name="grouped", align_bytes=64)
+            gv = grouped[:].rearrange("p (t m j) -> p m j t", t=PACK, j=PACK)
+            pieces = w1raw[b, a]
+            step = P // len(pieces)
+            for n, raw in enumerate(pieces):
+                src = raw[:].rearrange("p j (m t) -> p m j t", t=PACK)
+                dst = gv[:, n * step : (n + 1) * step]
+                if n == 0:
+                    nc.scalar.activation(out=dst, in_=src, func=ACT.Copy)
+                else:
+                    nc.vector.tensor_copy(out=dst, in_=src)
+            w1_w[b, a] = keep.tile([P, PASS], U32, name=f"w1w{b}_{a}", align_bytes=64)
+            w1_sc[b, a] = keep.tile([P, PASS], U8, name=f"w1s{b}_{a}", align_bytes=64)
+            cuts = [0, PASS] if len(pieces) == 1 else [0, P, 2 * P, PASS]
+            for lo, hi in zip(cuts[:-1], cuts[1:]):
+                nc.vector.quantize_mx(
+                    out=w1_w[b, a][:, lo:hi].bitcast(FP8X4),
+                    scales=w1_sc[b, a][:, lo:hi],
+                    in_=grouped[:, PACK * lo : PACK * hi],
+                )
+
+        def stage1(b, i):
+            acc = hps.tile([P, S], F32, name="hacc")
+            cols = slice(i * P, (i + 1) * P)
+            for a in range(KP):
+                nc.tensor.matmul_mx(
+                    out=acc[:],
+                    lhsT=w1_w[b, a][:, cols].bitcast(FP8X4),
+                    lhsT_scale=w1_sc[b, a][:, cols],
+                    rhs=v_w[a][:].bitcast(FP8X4),
+                    rhs_scale=v_sc[4 * a : P, :],
+                    start=(a == 0),
+                    stop=(a == KP - 1),
+                )
+            h = ring.tile([P, S], F32, name="h")
+            nc.scalar.copy(out=h[:], in_=acc[:])
+            return h
+
+        def scatter(i, h):
+            nc.vector.tensor_tensor(pages[i][:].indirect(list2[:]), h[:], wgs_sb[:], ALU.mult)
+
+        zb = {}
+
+        def add(b, i):
+            for u in range(2):
+                if i == 0:
+                    zb[b, u] = keep.tile([P, PACK, HALF], BF16, name=f"zb{b}_{u}")
+                cols = slice(u * HALF, (u + 1) * HALF)
+                nc.vector.tensor_tensor(zb[b, u][:, i, :], pages[i][:, cols], inv_sb[b, i][:, cols], ALU.add)
+
+        wc_w = {}
+        wc_sc = {}
+
+        def quant_wc(b):
+            grouped = ring.tile([P, PACK * N], BF16, name="grouped", align_bytes=64)
+            nc.scalar.activation(
+                out=grouped[:].rearrange("p (c e j) -> p c j e", e=4, j=PACK),
+                in_=wcraw[b][:].rearrange("p j (c e) -> p c j e", e=4),
+                func=ACT.Copy,
+                scale=-1.0,
+            )
+            wc_w[b] = keep.tile([P, N], U32, name=f"wcw{b}", align_bytes=64)
+            wc_sc[b] = keep.tile([P, N], U8, name=f"wcs{b}", align_bytes=64)
+            for lo, hi in ((0, 2 * P), (2 * P, N)):
+                nc.vector.quantize_mx(
+                    out=wc_w[b][:, lo:hi].bitcast(FP8X4),
+                    scales=wc_sc[b][:, lo:hi],
+                    in_=grouped[:, PACK * lo : PACK * hi],
+                )
+
+        def part(b, u, sign, on_vector):
+            g = ring.tile([P, PACK * HALF], BF16, name="part", align_bytes=64)
+            dst = g[:].rearrange("p (c e i) -> p c i e", e=4, i=PACK)
+            src = zb[b, u][:].rearrange("p i (c e) -> p c i e", e=4)
+            if on_vector:
+                nc.vector.tensor_scalar(dst, src, sign, 0.0, ALU.mult, ALU.max)
+            else:
+                nc.scalar.activation(out=dst, in_=src, func=ACT.Relu, scale=sign)
+            return g
+
+        def quant_part(g):
+            words = ring4.tile([P, HALF], U32, name="pw", align_bytes=64)
+            scales = ring4.tile([P, HALF], U8, name="psc", align_bytes=64)
+            nc.vector.quantize_mx(out=words[:].bitcast(FP8X4), scales=scales[:], in_=g[:])
+            return words, scales
+
+        oacc = {}
+
+        def mm_dis(b, u, ws, start, stop):
+            for nt in range(NT):
+                if start:
+                    oacc[nt, u] = ops.tile([P, HALF], F32, name=f"oacc{nt}_{u}")
+                c0 = b * N + nt * P
+                nc.tensor.matmul_mx(
+                    out=oacc[nt, u][:],
+                    lhsT=wd_w[:, 2 * c0 : 2 * (c0 + P)].bitcast(FP4X4),
+                    lhsT_scale=wd_sc[:, c0 : c0 + P],
+                    rhs=ws[0][:].bitcast(FP8X4),
+                    rhs_scale=ws[1][:],
+                    start=start,
+                    stop=stop,
+                )
+
+        def mm_chg(b, u, ws):
+            for nt in range(NT):
+                cols = slice(nt * P, (nt + 1) * P)
+                nc.tensor.matmul_mx(
+                    out=oacc[nt, u][:],
+                    lhsT=wc_w[b][:, cols].bitcast(FP8X4),
+                    lhsT_scale=wc_sc[b][:, cols],
+                    rhs=ws[0][:].bitcast(FP8X4),
+                    rhs_scale=ws[1][:],
+                    start=False,
+                    stop=False,
+                )
+
+        quant_w1(0, 0)
+        nc.vector.tensor_copy(v_w[1][:], tab[1][:].indirect(list1[:]))
+        quant_w1(0, 1)
+        nc.vector.tensor_copy(v_w[2][:], tab[2][:].indirect(list1[:]))
+        quant_w1(0, 2)
+
+        for i in range(PACK):
+            scatter(i, stage1(0, i))
+        for a in range(KP):
+            quant_w1(1, a)
+        for i in range(PACK):
+            add(0, i)
+        for i in range(PACK):
+            scatter(i, stage1(1, i))
+            if i == 0:
+                quant_wc(0)
+                quant_wc(1)
+            if i < 2:
+                dis = quant_part(part(0, i, 1.0, False))
+                mm_dis(0, i, dis, True, False)
+                chg = quant_part(part(0, i, -1.0, False))
+                mm_chg(0, i, chg)
+            add(1, i)
+
+        for u in range(2):
+            gd = part(1, u, 1.0, False)
+            gc = part(1, u, -1.0, True)
+            mm_chg(1, u, quant_part(gc))
+            mm_dis(1, u, quant_part(gd), False, True)
+            for nt in range(NT):
+                res = ring.tile([P, HALF], F32, name="res")
+                if u == 1 and nt == 1:
+                    nc.vector.tensor_copy(out=res[:], in_=oacc[nt, u][:])
+                else:
+                    nc.scalar.copy(out=res[:], in_=oacc[nt, u][:])
+                nc.sync.dma_start(out=out[nt * P : (nt + 1) * P, u * HALF : (u + 1) * HALF], in_=res[:])

@@ -1,6 +1,7 @@
 from contextlib import ExitStack
 
 import concourse.mybir as mybir
+from concourse.masks import make_identity
 
 K, T, S, T2, H, N = 1536, 2048, 512, 1024, 1024, 384
 FLOPS = 2 * K * H * S + 4 * H * N * T2
@@ -23,6 +24,7 @@ KP = K // PASS
 RP = H // PASS
 HALF = 512
 NT = N // P
+PAGES = 6
 
 
 def tile_list_battery_dispatch_split_kernel(
@@ -32,26 +34,28 @@ def tile_list_battery_dispatch_split_kernel(
     with ExitStack() as ctx:
         keep = ctx.enter_context(tc.tile_pool(name="keep", bufs=1))
         ring = ctx.enter_context(tc.tile_pool(name="ring", bufs=3))
-        ring4 = ctx.enter_context(tc.tile_pool(name="ring4", bufs=4))
-        hps = ctx.enter_context(tc.psum_pool(name="hps", bufs=2))
-        ops = ctx.enter_context(tc.psum_pool(name="ops", bufs=1))
+        ring6 = ctx.enter_context(tc.tile_pool(name="ring6", bufs=6))
+        psum = ctx.enter_context(tc.psum_pool(name="psum", bufs=1))
+        banks = [psum.tile([P, HALF], F32, name=f"bank{n}") for n in range(8)]
 
         list1 = keep.tile([P, S // 16], U16, name="list1")
         list2 = keep.tile([P, S // 16], U16, name="list2")
-        tab = [keep.tile([P, T], U32, name=f"tab{a}") for a in range(KP)]
+        tab = [keep.tile([P, T], U32, name=f"tab{a}", align_bytes=64) for a in range(KP)]
         tab_sc = keep.tile([P, T], U8, name="tab_sc", align_bytes=64)
         wd_sc = keep.tile([P, RP * N], U8, name="wd_sc", align_bytes=64)
         wd_w = keep.tile([P, RP * 2 * N], U8, name="wd_w", align_bytes=64)
         wgs_sb = keep.tile([P, S], F32, name="wgs_sb")
-        pages = [keep.tile([P, T2], F32, name=f"page{i}") for i in range(PACK)]
+        pages = [keep.tile([P, T2], F32, name=f"page{i}") for i in range(PAGES)]
 
+        ident = keep.tile([P, P], F32, name="ident")
+        make_identity(nc, ident[:])
         nc.vector.memset(tab_sc[:].bitcast(I32), 0)
         nc.vector.memset(wd_sc[:].bitcast(I32), 0)
         for page in pages:
             nc.vector.memset(page[:], 0.0)
 
         def load_w1(a, c0, width):
-            raw = keep.tile([P, PACK, width], F32, name=f"w1raw{a}_{c0}")
+            raw = keep.tile([P, PACK, width], F32, name=f"w1raw{a}_{c0}", align_bytes=64)
             rows = w1[a * PASS : (a + 1) * PASS, c0 : c0 + width]
             nc.sync.dma_start(out=raw[:], in_=rows.rearrange("(p j) c -> p j c", j=PACK))
             return raw
@@ -63,37 +67,37 @@ def tile_list_battery_dispatch_split_kernel(
 
         nc.sync.dma_start(list1[:], offs)
         load_tab(0)
+        w1raw = {}
+        w1raw[0, 0] = [load_w1(0, 0, PASS)]
         for q in range(4):
-            nc.scalar.dma_start(
+            nc.sync.dma_start(
                 out=tab_sc[32 * q : 32 * q + 4 * KP, :].bitcast(I32),
                 in_=tab_scales[:, 4 * q : 4 * q + 4, :].bitcast(I32),
             )
-        w1raw = {}
-        w1raw[0, 0] = [load_w1(0, 0, PASS)]
         load_tab(1)
         w1raw[0, 1] = [load_w1(1, 0, PASS)]
-        nc.sync.dma_start(list2[:], offs2)
-        nc.sync.dma_start(out=wgs_sb[:], in_=wgs)
         load_tab(2)
         w1raw[0, 2] = [load_w1(2, 0, PASS // 2), load_w1(2, PASS // 2, PASS // 2)]
+        nc.sync.dma_start(out=wgs_sb[:], in_=wgs)
+        nc.sync.dma_start(list2[:], offs2)
         for a in range(KP):
             w1raw[1, a] = [load_w1(a, PASS, PASS)]
 
         inv_sb = {}
 
         def load_inv(b):
-            rows = inv[b * PASS : (b + 1) * PASS, :].rearrange("(p j) m -> p j m", j=PACK)
-            for i in range(PACK):
-                inv_sb[b, i] = keep.tile([P, T2], F32, name=f"inv{b}_{i}")
-                nc.sync.dma_start(out=inv_sb[b, i][:], in_=rows[:, i, :])
+            rows = inv[b * PASS : (b + 1) * PASS, :].rearrange("(p u e) m -> p u (e m)", u=2, e=2)
+            for u in range(2):
+                inv_sb[b, u] = keep.tile([P, 2 * T2], F32, name=f"inv{b}_{u}")
+                nc.sync.dma_start(out=inv_sb[b, u][:], in_=rows[:, u, :])
 
-        load_inv(0)
         wcraw = []
         for b in range(RP):
-            wcraw.append(keep.tile([P, PACK, N], F32, name=f"wcraw{b}"))
+            wcraw.append(keep.tile([P, PACK, N], F32, name=f"wcraw{b}", align_bytes=64))
             nc.sync.dma_start(
                 out=wcraw[b][:], in_=wc[b * PASS : (b + 1) * PASS, :].rearrange("(p j) n -> p j n", j=PACK)
             )
+        load_inv(0)
         nc.sync.dma_start(
             out=wd_w[:].bitcast(I32).rearrange("p (b c) -> p b c", b=RP),
             in_=wd_words.bitcast(I32).rearrange("b p c -> p b c"),
@@ -124,7 +128,7 @@ def tile_list_battery_dispatch_split_kernel(
                 if n == 0:
                     nc.scalar.activation(out=dst, in_=src, func=ACT.Copy)
                 else:
-                    nc.vector.tensor_copy(out=dst, in_=src)
+                    nc.vector.tensor_copy(out=dst[:, :, :, 0], in_=src[:, :, :, 0])
             w1_w[b, a] = keep.tile([P, PASS], U32, name=f"w1w{b}_{a}", align_bytes=64)
             w1_sc[b, a] = keep.tile([P, PASS], U8, name=f"w1s{b}_{a}", align_bytes=64)
             cuts = [0, PASS] if len(pieces) == 1 else [0, P, 2 * P, PASS]
@@ -134,9 +138,11 @@ def tile_list_battery_dispatch_split_kernel(
                     scales=w1_sc[b, a][:, lo:hi],
                     in_=grouped[:, PACK * lo : PACK * hi],
                 )
+                if lo == 0 and hi < PASS:
+                    nc.vector.tensor_copy(out=dst[:, :, :, 1:], in_=src[:, :, :, 1:])
 
         def stage1(b, i):
-            acc = hps.tile([P, S], F32, name="hacc")
+            acc = banks[PACK * b + i]
             cols = slice(i * P, (i + 1) * P)
             for a in range(KP):
                 nc.tensor.matmul_mx(
@@ -148,86 +154,132 @@ def tile_list_battery_dispatch_split_kernel(
                     start=(a == 0),
                     stop=(a == KP - 1),
                 )
-            h = ring.tile([P, S], F32, name="h")
+            if (b, i) == (1, PACK - 1):
+                h = keep.tile([P, S], F32, name="h_last", tag="w1raw1_0", align_bytes=64)
+            else:
+                h = ring6.tile([P, S], F32, name="h", bufs=4)
             nc.scalar.copy(out=h[:], in_=acc[:])
             return h
 
-        def scatter(i, h):
-            nc.vector.tensor_tensor(pages[i][:].indirect(list2[:]), h[:], wgs_sb[:], ALU.mult)
+        def page_of(b, i):
+            return pages[(PACK * b + i) % PAGES]
 
-        zb = {}
+        def scatter(b, i, h):
+            nc.vector.tensor_tensor(page_of(b, i)[:].indirect(list2[:]), h[:], wgs_sb[:], ALU.mult)
 
-        def add(b, i):
-            for u in range(2):
-                if i == 0:
-                    zb[b, u] = keep.tile([P, PACK, HALF], BF16, name=f"zb{b}_{u}")
-                cols = slice(u * HALF, (u + 1) * HALF)
-                nc.vector.tensor_tensor(zb[b, u][:, i, :], pages[i][:, cols], inv_sb[b, i][:, cols], ALU.add)
+        turned = {}
+        woven = {}
 
-        wc_w = {}
-        wc_sc = {}
+        def sum_open(b, u, n, bank):
+            acc = banks[bank][:].rearrange("q (l e p) -> q l e p", l=2, e=2)
+            first = True
+            for e in range(2):
+                for l in range(2):
+                    m0 = (2 * n + l) * P
+                    nc.tensor.matmul(
+                        acc[:, l, e, :], lhsT=inv_sb[b, u][:, e * T2 + m0 : e * T2 + m0 + P], rhs=ident[:],
+                        is_transpose=True, start=first, stop=False,
+                    )
+                    first = False
+            for l in range(2):
+                m0 = (2 * n + l) * P
+                nc.tensor.matmul(
+                    acc[:, l, 0, :], lhsT=page_of(b, 2 * u)[:, m0 : m0 + P], rhs=ident[:],
+                    is_transpose=True, start=False, stop=False,
+                )
+            return acc
 
-        def quant_wc(b):
-            grouped = ring.tile([P, PACK * N], BF16, name="grouped", align_bytes=64)
-            nc.scalar.activation(
-                out=grouped[:].rearrange("p (c e j) -> p c j e", e=4, j=PACK),
-                in_=wcraw[b][:].rearrange("p j (c e) -> p c j e", e=4),
-                func=ACT.Copy,
-                scale=-1.0,
+        def sum_close(b, u, n, acc):
+            for l in range(2):
+                m0 = (2 * n + l) * P
+                nc.tensor.matmul(
+                    acc[:, l, 1, :], lhsT=page_of(b, 2 * u + 1)[:, m0 : m0 + P], rhs=ident[:],
+                    is_transpose=True, start=False, stop=(l == 1),
+                )
+            c0 = (u * 4 + n) * HALF
+            nc.scalar.copy(
+                out=turned[b][:, c0 : c0 + HALF].rearrange("q (l p e) -> q l p e", l=2, e=2),
+                in_=acc.rearrange("q l e p -> q l p e"),
             )
-            wc_w[b] = keep.tile([P, N], U32, name=f"wcw{b}", align_bytes=64)
-            wc_sc[b] = keep.tile([P, N], U8, name=f"wcs{b}", align_bytes=64)
-            for lo, hi in ((0, 2 * P), (2 * P, N)):
+
+        def turn_back(b, n, bank):
+            acc = banks[bank][:].rearrange("p (l u m) -> p l u m", l=2, u=2)
+            words = turned[b][:].bitcast(F32)
+            for u in range(2):
+                for l in range(2):
+                    c0 = (u * 8 + 2 * n + l) * P
+                    nc.tensor.transpose(acc[:, l, u, :], words[:, c0 : c0 + P], ident[:])
+            nc.scalar.copy(
+                out=woven[b][:].bitcast(F32)[:, n * HALF : (n + 1) * HALF].rearrange("p (l m u) -> p l m u", l=2, u=2),
+                in_=acc.rearrange("p l u m -> p l m u"),
+            )
+
+        wc_w = keep.tile([P, RP * N], U32, name="wc_w", align_bytes=64)
+        wc_sc = keep.tile([P, RP * N], U8, name="wc_sc", align_bytes=64)
+
+        def quant_wc():
+            grouped = keep.tile([P, RP * PACK * N], BF16, name="wc_grouped", align_bytes=64)
+            for b in range(RP):
+                nc.scalar.activation(
+                    out=grouped[:, b * PACK * N : (b + 1) * PACK * N].rearrange("p (c e j) -> p c j e", e=4, j=PACK),
+                    in_=wcraw[b][:].rearrange("p j (c e) -> p c j e", e=4),
+                    func=ACT.Copy,
+                    scale=-1.0,
+                )
+            for lo, hi in ((0, PASS), (PASS, RP * N)):
                 nc.vector.quantize_mx(
-                    out=wc_w[b][:, lo:hi].bitcast(FP8X4),
-                    scales=wc_sc[b][:, lo:hi],
+                    out=wc_w[:, lo:hi].bitcast(FP8X4),
+                    scales=wc_sc[:, lo:hi],
                     in_=grouped[:, PACK * lo : PACK * hi],
                 )
 
-        def part(b, u, sign, on_vector):
-            g = ring.tile([P, PACK * HALF], BF16, name="part", align_bytes=64)
-            dst = g[:].rearrange("p (c e i) -> p c i e", e=4, i=PACK)
-            src = zb[b, u][:].rearrange("p i (c e) -> p c i e", e=4)
-            if on_vector:
-                nc.vector.tensor_scalar(dst, src, sign, 0.0, ALU.mult, ALU.max)
+        def part(b, lo, hi, sign, on_scalar, tag):
+            g = keep.tile([P, PACK * (hi - lo)], BF16, name="part", tag=tag, align_bytes=64)
+            src = woven[b][:, PACK * lo : PACK * hi]
+            if on_scalar:
+                nc.scalar.activation(out=g[:], in_=src, func=ACT.Relu, scale=sign)
             else:
-                nc.scalar.activation(out=dst, in_=src, func=ACT.Relu, scale=sign)
+                nc.vector.tensor_scalar(g[:], src, sign, 0.0, ALU.mult, ALU.max)
             return g
 
-        def quant_part(g):
-            words = ring4.tile([P, HALF], U32, name="pw", align_bytes=64)
-            scales = ring4.tile([P, HALF], U8, name="psc", align_bytes=64)
-            nc.vector.quantize_mx(out=words[:].bitcast(FP8X4), scales=scales[:], in_=g[:])
-            return words, scales
+        codes = {}
 
-        oacc = {}
-
-        def mm_dis(b, u, ws, start, stop):
-            for nt in range(NT):
-                if start:
-                    oacc[nt, u] = ops.tile([P, HALF], F32, name=f"oacc{nt}_{u}")
-                c0 = b * N + nt * P
-                nc.tensor.matmul_mx(
-                    out=oacc[nt, u][:],
-                    lhsT=wd_w[:, 2 * c0 : 2 * (c0 + P)].bitcast(FP4X4),
-                    lhsT_scale=wd_sc[:, c0 : c0 + P],
-                    rhs=ws[0][:].bitcast(FP8X4),
-                    rhs_scale=ws[1][:],
-                    start=start,
-                    stop=stop,
+        def quant_part(name, g, lo, cuts, tag=None):
+            width = cuts[-1] - lo
+            words = keep.tile([P, width], U32, name=f"{name}_w{lo}", tag=tag or f"{name}_w{lo}", align_bytes=64)
+            scales = keep.tile([P, width], U8, name=f"{name}_sc{lo}", align_bytes=64)
+            for c0 in range(lo, cuts[-1], P):
+                codes[name, c0] = (words, scales, lo)
+            for c0, c1 in zip(cuts[:-1], cuts[1:]):
+                nc.vector.quantize_mx(
+                    out=words[:, c0 - lo : c1 - lo].bitcast(FP8X4),
+                    scales=scales[:, c0 - lo : c1 - lo],
+                    in_=g[:, PACK * (c0 - lo) : PACK * (c1 - lo)],
                 )
 
-        def mm_chg(b, u, ws):
-            for nt in range(NT):
-                cols = slice(nt * P, (nt + 1) * P)
+        def mm(name, b, nt, dst, lo, hi, start=False, stop=False):
+            c0 = b * N + nt * P
+            if name == "dis":
+                lhsT, lhsT_scale = wd_w[:, 2 * c0 : 2 * (c0 + P)].bitcast(FP4X4), wd_sc[:, c0 : c0 + P]
+            else:
+                lhsT, lhsT_scale = wc_w[:, c0 : c0 + P].bitcast(FP8X4), wc_sc[:, c0 : c0 + P]
+            width = hi - lo
+            if width == HALF:
+                cuts = [0, width]
+            elif name == "chg" and width == 3 * P:
+                cuts = [0, 2 * P, width]
+            else:
+                cuts = list(range(0, width + 1, P))
+            for c1, c2 in zip(cuts[:-1], cuts[1:]):
+                words, scales, base = codes[f"{name}{b}", lo + c1]
                 nc.tensor.matmul_mx(
-                    out=oacc[nt, u][:],
-                    lhsT=wc_w[b][:, cols].bitcast(FP8X4),
-                    lhsT_scale=wc_sc[b][:, cols],
-                    rhs=ws[0][:].bitcast(FP8X4),
-                    rhs_scale=ws[1][:],
-                    start=False,
-                    stop=False,
+                    out=dst[:, c1:c2],
+                    lhsT=lhsT,
+                    lhsT_scale=lhsT_scale,
+                    rhs=words[:, lo - base + c1 : lo - base + c2].bitcast(FP8X4),
+                    rhs_scale=scales[:, lo - base + c1 : lo - base + c2],
+                    start=start and c1 == 0,
+                    stop=stop and c2 == width,
                 )
 
         quant_w1(0, 0)
@@ -236,33 +288,123 @@ def tile_list_battery_dispatch_split_kernel(
         nc.vector.tensor_copy(v_w[2][:], tab[2][:].indirect(list1[:]))
         quant_w1(0, 2)
 
+        turned[0] = keep.tile([P, PACK * T2], BF16, name="turned0", tag="tab0", align_bytes=64)
+        turned[1] = keep.tile([P, 2 * T2], BF16, name="turned1", tag="tab2", align_bytes=64)
+        woven[0] = keep.tile([P, PACK * T2], BF16, name="woven0", tag="tab1", align_bytes=64)
+        pairs = keep.tile([P, PACK * T2], BF16, name="pairs", tag="w1raw0_0", align_bytes=64)
+
+        def sum_block(b, u, n, bank):
+            sum_close(b, u, n, sum_open(b, u, n, bank))
+
+        def pair_back(n, bank):
+            acc = banks[bank]
+            words = turned[1][:].bitcast(F32)
+            for l in range(4):
+                c0 = (4 * n + l) * P
+                nc.tensor.transpose(acc[:, l * P : (l + 1) * P], words[:, c0 : c0 + P], ident[:])
+            nc.scalar.copy(out=pairs[:].bitcast(F32)[:, n * HALF : (n + 1) * HALF], in_=acc[:])
+
+        def add_plane(i, lo, hi):
+            e = i % 2
+            dst = pairs[:].rearrange("p (u m e) -> p u m e", u=2, e=2)[:, 1, lo:hi, e]
+            nc.vector.tensor_tensor(dst, page_of(1, i)[:, lo:hi], inv_sb[1, 1][:, e * T2 + lo : e * T2 + hi], ALU.add)
+
+        def part1(lo, hi, sign, on_scalar, tag):
+            g = keep.tile([P, PACK * (hi - lo)], BF16, name="part1", tag=tag, align_bytes=64)
+            dst = g[:].rearrange("p (m u e) -> p m u e", u=2, e=2)
+            src = pairs[:].rearrange("p (u m e) -> p m u e", u=2, e=2)[:, lo:hi]
+            if on_scalar:
+                nc.scalar.activation(out=dst, in_=src, func=ACT.Relu, scale=sign)
+            else:
+                nc.vector.tensor_scalar(dst, src, sign, 0.0, ALU.mult, ALU.max)
+            return g
+
+        X0, Y0, Z0 = 0, HALF, T2 - P
         for i in range(PACK):
-            scatter(i, stage1(0, i))
+            scatter(0, i, stage1(0, i))
         for a in range(KP):
             quant_w1(1, a)
-        for i in range(PACK):
-            add(0, i)
-        for i in range(PACK):
-            scatter(i, stage1(1, i))
-            if i == 0:
-                quant_wc(0)
-                quant_wc(1)
-            if i < 2:
-                dis = quant_part(part(0, i, 1.0, False))
-                mm_dis(0, i, dis, True, False)
-                chg = quant_part(part(0, i, -1.0, False))
-                mm_chg(0, i, chg)
-            add(1, i)
+        quant_wc()
+        for n in range(3):
+            sum_block(0, 0, n, 4 + n)
+        scatter(1, 0, stage1(1, 0))
+        sum_block(0, 0, 3, 7)
+        for n in range(2):
+            sum_block(0, 1, n, n)
+        scatter(1, 1, stage1(1, 1))
+        for n in range(2, 4):
+            sum_block(0, 1, n, n)
+        scatter(1, 2, stage1(1, 2))
+        for n in range(4):
+            turn_back(0, n, n)
+        for lo in (0, HALF):
+            add_plane(2, lo, lo + HALF)
+        dis_a = part(0, X0, Y0, 1.0, True, "w1raw1_0")
+        dis_b = part(0, Y0, T2, 1.0, True, "w1raw2_0")
+        chg0 = part(0, 0, T2, -1.0, False, "w1raw0_512")
+        quant_part("dis0", dis_a, X0, [X0, Y0], tag="tab0")
+        quant_part("chg0", chg0, X0, [X0, T2])
+        for n in range(4):
+            sum_block(1, 0, n, n)
+        h_last = stage1(1, 3)
+        for n in range(2):
+            pair_back(n, 4 + n)
+        quant_part("dis0", dis_b, Y0, [Y0, T2], tag="tab2")
+        scatter(1, 3, h_last)
+        acc = {}
+        for m0, bank in zip(range(0, T2, P), (3, 4, 5, 7, 0, 1, 2, 6)):
+            acc[m0] = banks[bank][:, : NT * P].rearrange("p (t m) -> p t m", t=NT)
 
-        for u in range(2):
-            gd = part(1, u, 1.0, False)
-            gc = part(1, u, -1.0, True)
-            mm_chg(1, u, quant_part(gc))
-            mm_dis(1, u, quant_part(gd), False, True)
+        def mm_narrow(name, b, m0, start=False, stop=False):
             for nt in range(NT):
-                res = ring.tile([P, HALF], F32, name="res")
-                if u == 1 and nt == 1:
-                    nc.vector.tensor_copy(out=res[:], in_=oacc[nt, u][:])
+                mm(name, b, nt, acc[m0][:, nt, :], m0, m0 + P, start=start and nt == 0, stop=stop and nt == NT - 1)
+
+        for m0 in range(0, T2, P):
+            mm_narrow("dis", 0, m0, start=True)
+            mm_narrow("chg", 0, m0)
+
+        def store(m0, width, on_vector):
+            res = ring6.tile([P, NT, width], F32, name="res", bufs=5)
+            for c0 in range(0, width, P):
+                if on_vector[c0 // P]:
+                    nc.vector.tensor_copy(out=res[:, :, c0 : c0 + P], in_=acc[m0 + c0])
                 else:
-                    nc.scalar.copy(out=res[:], in_=oacc[nt, u][:])
-                nc.sync.dma_start(out=out[nt * P : (nt + 1) * P, u * HALF : (u + 1) * HALF], in_=res[:])
+                    nc.scalar.copy(out=res[:, :, c0 : c0 + P], in_=acc[m0 + c0])
+            nc.sync.dma_start(out=out[:, m0 : m0 + width].rearrange("(t p) m -> p t m", p=P), in_=res[:])
+
+        Q = 2 * P
+        free_tags = ["w1raw2_256", "w1raw2_512", "w1raw1_512", "wcraw0", "wcraw1", "wc_grouped", "tab1", "w1raw0_512"]
+        parts = {}
+
+        def make(k):
+            parts[k] = (
+                part1(k * Q, (k + 1) * Q, 1.0, k in (0, 1, 2), free_tags[2 * k]),
+                part1(k * Q, (k + 1) * Q, -1.0, False, free_tags[2 * k + 1]),
+            )
+
+        def finish(k):
+            lo = k * Q
+            last = k == 3
+            quant_part("chg1", parts[k][1], lo, [lo, lo + Q])
+            quant_part("dis1", parts[k][0], lo, [lo, lo + P, lo + Q] if last else [lo, lo + Q])
+            for m0 in (lo, lo + P):
+                mm_narrow("chg", 1, m0)
+            for m0 in (lo, lo + P):
+                mm_narrow("dis", 1, m0, stop=True)
+            if last:
+                store(lo, P, (True,))
+                store(lo + P, P, (False,))
+            else:
+                store(lo, Q, (False, False))
+
+        add_plane(3, 0, Q)
+        add_plane(3, Q, 2 * Q)
+        make(0)
+        add_plane(3, 2 * Q, T2)
+        finish(0)
+        make(1)
+        make(2)
+        finish(1)
+        make(3)
+        finish(2)
+        finish(3)

@@ -20,11 +20,15 @@ ACT = mybir.ActivationFunctionType
 P = 128
 PACK = 4
 PASS = P * PACK
-KP = K // PASS
-RP = H // PASS
-HALF = 512
-NT = N // P
+K_PASSES = K // PASS
+R_PASSES = H // PASS
+N_TILES = N // P
+BANK = 512
+QUADRANTS = 4
+HALF = T2 // 2
+QUARTER = T2 // 4
 PAGES = 6
+QUARTERS_ON_SCALAR = 3
 
 
 def tile_list_battery_dispatch_split_kernel(
@@ -33,19 +37,19 @@ def tile_list_battery_dispatch_split_kernel(
     nc = tc.nc
     with ExitStack() as ctx:
         keep = ctx.enter_context(tc.tile_pool(name="keep", bufs=1))
-        ring = ctx.enter_context(tc.tile_pool(name="ring", bufs=3))
-        ring6 = ctx.enter_context(tc.tile_pool(name="ring6", bufs=6))
+        casts = ctx.enter_context(tc.tile_pool(name="casts", bufs=3))
+        ring = ctx.enter_context(tc.tile_pool(name="ring", bufs=4))
         psum = ctx.enter_context(tc.psum_pool(name="psum", bufs=1))
-        banks = [psum.tile([P, HALF], F32, name=f"bank{n}") for n in range(8)]
+        banks = [psum.tile([P, BANK], F32, name=f"bank{n}") for n in range(8)]
 
-        list1 = keep.tile([P, S // 16], U16, name="list1")
-        list2 = keep.tile([P, S // 16], U16, name="list2")
-        tab = [keep.tile([P, T], U32, name=f"tab{a}", align_bytes=64) for a in range(KP)]
+        zones = keep.tile([P, S // 16], U16, name="zones")
+        places = keep.tile([P, S // 16], U16, name="places")
+        tab_w = [keep.tile([P, T], U32, name=f"tab{a}", align_bytes=64) for a in range(K_PASSES)]
         tab_sc = keep.tile([P, T], U8, name="tab_sc", align_bytes=64)
-        wd_sc = keep.tile([P, RP * N], U8, name="wd_sc", align_bytes=64)
-        wd_w = keep.tile([P, RP * 2 * N], U8, name="wd_w", align_bytes=64)
+        wd_sc = keep.tile([P, R_PASSES * N], U8, name="wd_sc", align_bytes=64)
+        wd_w = keep.tile([P, R_PASSES * 2 * N], U8, name="wd_w", align_bytes=64)
         wgs_sb = keep.tile([P, S], F32, name="wgs_sb")
-        pages = [keep.tile([P, T2], F32, name=f"page{i}") for i in range(PAGES)]
+        pages = [keep.tile([P, T2], F32, name=f"page{n}") for n in range(PAGES)]
 
         ident = keep.tile([P, P], F32, name="ident")
         make_identity(nc, ident[:])
@@ -54,357 +58,307 @@ def tile_list_battery_dispatch_split_kernel(
         for page in pages:
             nc.vector.memset(page[:], 0.0)
 
-        def load_w1(a, c0, width):
-            raw = keep.tile([P, PACK, width], F32, name=f"w1raw{a}_{c0}", align_bytes=64)
-            rows = w1[a * PASS : (a + 1) * PASS, c0 : c0 + width]
-            nc.sync.dma_start(out=raw[:], in_=rows.rearrange("(p j) c -> p j c", j=PACK))
-            return raw
+        w1_raw = {}
+        inv_sb = {}
+        wc_raw = {}
 
         def load_tab(a):
             nc.sync.dma_start(
-                out=tab[a][:].bitcast(I32), in_=tab_words[a].rearrange("p t i -> p (t i)").bitcast(I32)
+                out=tab_w[a][:].bitcast(I32), in_=tab_words[a].rearrange("p t i -> p (t i)").bitcast(I32)
             )
 
-        nc.sync.dma_start(list1[:], offs)
-        load_tab(0)
-        w1raw = {}
-        w1raw[0, 0] = [load_w1(0, 0, PASS)]
-        for q in range(4):
+        def load_w1(b, a, pieces=1):
+            width = PASS // pieces
+            w1_raw[b, a] = []
+            for c0 in range(b * PASS, (b + 1) * PASS, width):
+                raw = keep.tile([P, PACK, width], F32, name=f"w1_k{a}_r{c0}", align_bytes=64)
+                rows = w1[a * PASS : (a + 1) * PASS, c0 : c0 + width]
+                nc.sync.dma_start(out=raw[:], in_=rows.rearrange("(p j) c -> p j c", j=PACK))
+                w1_raw[b, a].append(raw)
+
+        def load_inv(b, u):
+            rows = inv[b * PASS : (b + 1) * PASS, :].rearrange("(p u e) m -> p u (e m)", u=2, e=2)
+            inv_sb[b, u] = keep.tile([P, 2 * T2], F32, name=f"inv{b}_{u}")
+            nc.sync.dma_start(out=inv_sb[b, u][:], in_=rows[:, u, :])
+
+        def load_wc(b):
+            wc_raw[b] = keep.tile([P, PACK, N], F32, name=f"wc_raw{b}", align_bytes=64)
             nc.sync.dma_start(
-                out=tab_sc[32 * q : 32 * q + 4 * KP, :].bitcast(I32),
+                out=wc_raw[b][:], in_=wc[b * PASS : (b + 1) * PASS, :].rearrange("(p j) n -> p j n", j=PACK)
+            )
+
+        nc.sync.dma_start(zones[:], offs)
+        load_tab(0)
+        load_w1(0, 0)
+        for q in range(QUADRANTS):
+            nc.sync.dma_start(
+                out=tab_sc[32 * q : 32 * q + 4 * K_PASSES, :].bitcast(I32),
                 in_=tab_scales[:, 4 * q : 4 * q + 4, :].bitcast(I32),
             )
         load_tab(1)
-        w1raw[0, 1] = [load_w1(1, 0, PASS)]
+        load_w1(0, 1)
         load_tab(2)
-        w1raw[0, 2] = [load_w1(2, 0, PASS // 2), load_w1(2, PASS // 2, PASS // 2)]
+        load_w1(0, 2, pieces=2)
         nc.sync.dma_start(out=wgs_sb[:], in_=wgs)
-        nc.sync.dma_start(list2[:], offs2)
-        for a in range(KP):
-            w1raw[1, a] = [load_w1(a, PASS, PASS)]
-
-        inv_sb = {}
-
-        def load_inv(b):
-            rows = inv[b * PASS : (b + 1) * PASS, :].rearrange("(p u e) m -> p u (e m)", u=2, e=2)
-            for u in range(2):
-                inv_sb[b, u] = keep.tile([P, 2 * T2], F32, name=f"inv{b}_{u}")
-                nc.sync.dma_start(out=inv_sb[b, u][:], in_=rows[:, u, :])
-
-        wcraw = []
-        for b in range(RP):
-            wcraw.append(keep.tile([P, PACK, N], F32, name=f"wcraw{b}", align_bytes=64))
-            nc.sync.dma_start(
-                out=wcraw[b][:], in_=wc[b * PASS : (b + 1) * PASS, :].rearrange("(p j) n -> p j n", j=PACK)
-            )
-        load_inv(0)
+        nc.sync.dma_start(places[:], offs2)
+        for a in range(K_PASSES):
+            load_w1(1, a)
+        load_inv(0, 0)
+        for b in range(R_PASSES):
+            load_wc(b)
+        load_inv(0, 1)
         nc.sync.dma_start(
-            out=wd_w[:].bitcast(I32).rearrange("p (b c) -> p b c", b=RP),
+            out=wd_w[:].bitcast(I32).rearrange("p (b c) -> p b c", b=R_PASSES),
             in_=wd_words.bitcast(I32).rearrange("b p c -> p b c"),
         )
-        for q in range(4):
+        for q in range(QUADRANTS):
             nc.sync.dma_start(
-                out=wd_sc[32 * q : 32 * q + 4, :].bitcast(I32).rearrange("r (b c) -> r b c", b=RP),
-                in_=wd_scales[:, 4 * q : 4 * q + 4, :].bitcast(I32).rearrange("b r c -> r b c"),
+                out=wd_sc[32 * q : 32 * q + 4, :].bitcast(I32).rearrange("s (b c) -> s b c", b=R_PASSES),
+                in_=wd_scales[:, 4 * q : 4 * q + 4, :].bitcast(I32).rearrange("b s c -> s b c"),
             )
-        load_inv(1)
+        for u in range(2):
+            load_inv(1, u)
 
         v_sc = keep.tile([P, S], U8, name="v_sc", align_bytes=64)
-        v_w = [keep.tile([P, S], U32, name=f"v_w{a}", align_bytes=64) for a in range(KP)]
-        nc.vector.tensor_copy(v_w[0][:], tab[0][:].indirect(list1[:]))
-        nc.vector.tensor_copy(v_sc[:], tab_sc[:].indirect(list1[:]))
-
+        v_w = [keep.tile([P, S], U32, name=f"v_w{a}", align_bytes=64) for a in range(K_PASSES)]
         w1_w = {}
         w1_sc = {}
 
-        def quant_w1(b, a):
-            grouped = ring.tile([P, PACK * PASS], BF16, name="grouped", align_bytes=64)
-            gv = grouped[:].rearrange("p (t m j) -> p m j t", t=PACK, j=PACK)
-            pieces = w1raw[b, a]
-            step = P // len(pieces)
-            for n, raw in enumerate(pieces):
-                src = raw[:].rearrange("p j (m t) -> p m j t", t=PACK)
-                dst = gv[:, n * step : (n + 1) * step]
-                if n == 0:
-                    nc.scalar.activation(out=dst, in_=src, func=ACT.Copy)
-                else:
-                    nc.vector.tensor_copy(out=dst[:, :, :, 0], in_=src[:, :, :, 0])
-            w1_w[b, a] = keep.tile([P, PASS], U32, name=f"w1w{b}_{a}", align_bytes=64)
-            w1_sc[b, a] = keep.tile([P, PASS], U8, name=f"w1s{b}_{a}", align_bytes=64)
-            cuts = [0, PASS] if len(pieces) == 1 else [0, P, 2 * P, PASS]
-            for lo, hi in zip(cuts[:-1], cuts[1:]):
-                nc.vector.quantize_mx(
-                    out=w1_w[b, a][:, lo:hi].bitcast(FP8X4),
-                    scales=w1_sc[b, a][:, lo:hi],
-                    in_=grouped[:, PACK * lo : PACK * hi],
-                )
-                if lo == 0 and hi < PASS:
-                    nc.vector.tensor_copy(out=dst[:, :, :, 1:], in_=src[:, :, :, 1:])
+        def quantize(words, scales, values, lo, hi):
+            nc.vector.quantize_mx(
+                out=words[:, lo:hi].bitcast(FP8X4), scales=scales[:, lo:hi], in_=values[:, PACK * lo : PACK * hi]
+            )
 
-        def stage1(b, i):
-            acc = banks[PACK * b + i]
+        def quantize_w1(b, a):
+            cast = casts.tile([P, PACK * PASS], BF16, name="w1_cast", align_bytes=64)
+            dst = cast[:].rearrange("p (i m j) -> p m j i", i=PACK, j=PACK)
+            src = [raw[:].rearrange("p j (m i) -> p m j i", i=PACK) for raw in w1_raw[b, a]]
+            w1_w[b, a] = keep.tile([P, PASS], U32, name=f"w1_w{b}_{a}", align_bytes=64)
+            w1_sc[b, a] = keep.tile([P, PASS], U8, name=f"w1_sc{b}_{a}", align_bytes=64)
+            if len(src) == 1:
+                nc.scalar.activation(out=dst, in_=src[0], func=ACT.Copy)
+                quantize(w1_w[b, a], w1_sc[b, a], cast, 0, PASS)
+            else:
+                nc.scalar.activation(out=dst[:, : P // 2], in_=src[0], func=ACT.Copy)
+                nc.vector.tensor_copy(out=dst[:, P // 2 :, :, 0], in_=src[1][:, :, :, 0])
+                quantize(w1_w[b, a], w1_sc[b, a], cast, 0, P)
+                nc.vector.tensor_copy(out=dst[:, P // 2 :, :, 1:], in_=src[1][:, :, :, 1:])
+                quantize(w1_w[b, a], w1_sc[b, a], cast, P, 2 * P)
+                quantize(w1_w[b, a], w1_sc[b, a], cast, 2 * P, PASS)
+
+        def first_product(b, i, h):
+            bank = banks[PACK * b + i]
             cols = slice(i * P, (i + 1) * P)
-            for a in range(KP):
+            for a in range(K_PASSES):
                 nc.tensor.matmul_mx(
-                    out=acc[:],
+                    out=bank[:],
                     lhsT=w1_w[b, a][:, cols].bitcast(FP8X4),
                     lhsT_scale=w1_sc[b, a][:, cols],
                     rhs=v_w[a][:].bitcast(FP8X4),
                     rhs_scale=v_sc[4 * a : P, :],
                     start=(a == 0),
-                    stop=(a == KP - 1),
+                    stop=(a == K_PASSES - 1),
                 )
-            if (b, i) == (1, PACK - 1):
-                h = keep.tile([P, S], F32, name="h_last", tag="w1raw1_0", align_bytes=64)
-            else:
-                h = ring6.tile([P, S], F32, name="h", bufs=4)
-            nc.scalar.copy(out=h[:], in_=acc[:])
-            return h
+            nc.scalar.copy(out=h[:], in_=bank[:])
 
         def page_of(b, i):
             return pages[(PACK * b + i) % PAGES]
 
         def scatter(b, i, h):
-            nc.vector.tensor_tensor(page_of(b, i)[:].indirect(list2[:]), h[:], wgs_sb[:], ALU.mult)
+            nc.vector.tensor_tensor(page_of(b, i)[:].indirect(places[:]), h[:], wgs_sb[:], ALU.mult)
 
-        turned = {}
-        woven = {}
+        def product_and_scatter(b, i):
+            h = ring.tile([P, S], F32, name="h")
+            first_product(b, i, h)
+            scatter(b, i, h)
 
-        def sum_open(b, u, n, bank):
-            acc = banks[bank][:].rearrange("q (l e p) -> q l e p", l=2, e=2)
-            first = True
-            for e in range(2):
+        for a in range(K_PASSES):
+            nc.vector.tensor_copy(v_w[a][:], tab_w[a][:].indirect(zones[:]))
+            if a == 0:
+                nc.vector.tensor_copy(v_sc[:], tab_sc[:].indirect(zones[:]))
+            quantize_w1(0, a)
+
+        turned = [
+            keep.tile([P, PACK * T2], BF16, name="turned0", tag="tab0", align_bytes=64),
+            keep.tile([P, 2 * T2], BF16, name="turned1", tag="tab2", align_bytes=64),
+        ]
+        z0 = keep.tile([P, PACK * T2], BF16, name="z0", tag="tab1", align_bytes=64)
+        z1 = keep.tile([P, PACK * T2], BF16, name="z1", tag="w1_k0_r0", align_bytes=64)
+
+        def sum_quarter(b, u, n, bank):
+            acc = bank[:].rearrange("q (l e p) -> q l e p", l=2, e=2)
+            planes = [(e, inv_sb[b, u][:, e * T2 : (e + 1) * T2]) for e in range(2)]
+            planes += [(e, page_of(b, 2 * u + e)[:]) for e in range(2)]
+            for step, (e, plane) in enumerate(planes):
                 for l in range(2):
-                    m0 = (2 * n + l) * P
+                    m0 = n * QUARTER + l * P
                     nc.tensor.matmul(
-                        acc[:, l, e, :], lhsT=inv_sb[b, u][:, e * T2 + m0 : e * T2 + m0 + P], rhs=ident[:],
-                        is_transpose=True, start=first, stop=False,
+                        acc[:, l, e, :],
+                        lhsT=plane[:, m0 : m0 + P],
+                        rhs=ident[:],
+                        is_transpose=True,
+                        start=(step == 0 and l == 0),
+                        stop=(step == len(planes) - 1 and l == 1),
                     )
-                    first = False
-            for l in range(2):
-                m0 = (2 * n + l) * P
-                nc.tensor.matmul(
-                    acc[:, l, 0, :], lhsT=page_of(b, 2 * u)[:, m0 : m0 + P], rhs=ident[:],
-                    is_transpose=True, start=False, stop=False,
-                )
-            return acc
-
-        def sum_close(b, u, n, acc):
-            for l in range(2):
-                m0 = (2 * n + l) * P
-                nc.tensor.matmul(
-                    acc[:, l, 1, :], lhsT=page_of(b, 2 * u + 1)[:, m0 : m0 + P], rhs=ident[:],
-                    is_transpose=True, start=False, stop=(l == 1),
-                )
-            c0 = (u * 4 + n) * HALF
+            c0 = 2 * (u * T2 + n * QUARTER)
             nc.scalar.copy(
-                out=turned[b][:, c0 : c0 + HALF].rearrange("q (l p e) -> q l p e", l=2, e=2),
+                out=turned[b][:, c0 : c0 + 2 * QUARTER].rearrange("q (l p e) -> q l p e", l=2, e=2),
                 in_=acc.rearrange("q l e p -> q l p e"),
             )
 
-        def turn_back(b, n, bank):
-            acc = banks[bank][:].rearrange("p (l u m) -> p l u m", l=2, u=2)
-            words = turned[b][:].bitcast(F32)
+        def turn_back_pass0(n, bank):
+            acc = bank[:].rearrange("p (l u m) -> p l u m", l=2, u=2)
+            words = turned[0][:].bitcast(F32)
             for u in range(2):
                 for l in range(2):
-                    c0 = (u * 8 + 2 * n + l) * P
+                    c0 = u * T2 + n * QUARTER + l * P
                     nc.tensor.transpose(acc[:, l, u, :], words[:, c0 : c0 + P], ident[:])
+            dst = z0[:].bitcast(F32)[:, 2 * n * QUARTER : 2 * (n + 1) * QUARTER]
             nc.scalar.copy(
-                out=woven[b][:].bitcast(F32)[:, n * HALF : (n + 1) * HALF].rearrange("p (l m u) -> p l m u", l=2, u=2),
-                in_=acc.rearrange("p l u m -> p l m u"),
+                out=dst.rearrange("p (l m u) -> p l m u", l=2, u=2), in_=acc.rearrange("p l u m -> p l m u")
             )
 
-        wc_w = keep.tile([P, RP * N], U32, name="wc_w", align_bytes=64)
-        wc_sc = keep.tile([P, RP * N], U8, name="wc_sc", align_bytes=64)
+        def turn_back_pass1(n, bank):
+            words = turned[1][:].bitcast(F32)
+            for c0 in range(0, HALF, P):
+                nc.tensor.transpose(bank[:, c0 : c0 + P], words[:, n * HALF + c0 : n * HALF + c0 + P], ident[:])
+            nc.scalar.copy(out=z1[:].bitcast(F32)[:, n * HALF : (n + 1) * HALF], in_=bank[:])
 
-        def quant_wc():
-            grouped = keep.tile([P, RP * PACK * N], BF16, name="wc_grouped", align_bytes=64)
-            for b in range(RP):
+        def add_last_pair(e, lo, hi):
+            dst = z1[:].rearrange("p (u m e) -> p u m e", u=2, e=2)[:, 1, lo:hi, e]
+            nc.vector.tensor_tensor(
+                dst, page_of(1, 2 + e)[:, lo:hi], inv_sb[1, 1][:, e * T2 + lo : e * T2 + hi], ALU.add
+            )
+
+        SIGN = {"dis": 1.0, "chg": -1.0}
+        wc_w = keep.tile([P, R_PASSES * N], U32, name="wc_w", align_bytes=64)
+        wc_sc = keep.tile([P, R_PASSES * N], U8, name="wc_sc", align_bytes=64)
+        codes = {}
+
+        def quantize_wc():
+            cast = keep.tile([P, R_PASSES * PACK * N], BF16, name="wc_cast", align_bytes=64)
+            for b in range(R_PASSES):
                 nc.scalar.activation(
-                    out=grouped[:, b * PACK * N : (b + 1) * PACK * N].rearrange("p (c e j) -> p c j e", e=4, j=PACK),
-                    in_=wcraw[b][:].rearrange("p j (c e) -> p c j e", e=4),
+                    out=cast[:, b * PACK * N : (b + 1) * PACK * N].rearrange("p (c e j) -> p c j e", e=4, j=PACK),
+                    in_=wc_raw[b][:].rearrange("p j (c e) -> p c j e", e=4),
                     func=ACT.Copy,
                     scale=-1.0,
                 )
-            for lo, hi in ((0, PASS), (PASS, RP * N)):
-                nc.vector.quantize_mx(
-                    out=wc_w[:, lo:hi].bitcast(FP8X4),
-                    scales=wc_sc[:, lo:hi],
-                    in_=grouped[:, PACK * lo : PACK * hi],
-                )
+            quantize(wc_w, wc_sc, cast, 0, PASS)
+            quantize(wc_w, wc_sc, cast, PASS, R_PASSES * N)
 
-        def part(b, lo, hi, sign, on_scalar, tag):
-            g = keep.tile([P, PACK * (hi - lo)], BF16, name="part", tag=tag, align_bytes=64)
-            src = woven[b][:, PACK * lo : PACK * hi]
+        def part(name, b, lo, hi, on_scalar, tag):
+            values = keep.tile([P, PACK * (hi - lo)], BF16, name=f"{name}{b}_{lo}", tag=tag, align_bytes=64)
+            if b == 0:
+                dst, src = values[:], z0[:, PACK * lo : PACK * hi]
+            else:
+                dst = values[:].rearrange("p (m u e) -> p m u e", u=2, e=2)
+                src = z1[:].rearrange("p (u m e) -> p m u e", u=2, e=2)[:, lo:hi]
             if on_scalar:
-                nc.scalar.activation(out=g[:], in_=src, func=ACT.Relu, scale=sign)
+                nc.scalar.activation(out=dst, in_=src, func=ACT.Relu, scale=SIGN[name])
             else:
-                nc.vector.tensor_scalar(g[:], src, sign, 0.0, ALU.mult, ALU.max)
-            return g
+                nc.vector.tensor_scalar(dst, src, SIGN[name], 0.0, ALU.mult, ALU.max)
+            return values
 
-        codes = {}
+        def quantize_part(name, b, values, lo, widths, tag=None):
+            own = f"{name}{b}_w{lo}"
+            words = keep.tile([P, sum(widths)], U32, name=own, tag=tag or own, align_bytes=64)
+            scales = keep.tile([P, sum(widths)], U8, name=f"{name}{b}_sc{lo}", align_bytes=64)
+            for c0 in range(0, sum(widths), P):
+                codes[name, b, lo + c0] = (words[:, c0 : c0 + P], scales[:, c0 : c0 + P])
+            for n, width in enumerate(widths):
+                quantize(words, scales, values, sum(widths[:n]), sum(widths[:n]) + width)
 
-        def quant_part(name, g, lo, cuts, tag=None):
-            width = cuts[-1] - lo
-            words = keep.tile([P, width], U32, name=f"{name}_w{lo}", tag=tag or f"{name}_w{lo}", align_bytes=64)
-            scales = keep.tile([P, width], U8, name=f"{name}_sc{lo}", align_bytes=64)
-            for c0 in range(lo, cuts[-1], P):
-                codes[name, c0] = (words, scales, lo)
-            for c0, c1 in zip(cuts[:-1], cuts[1:]):
-                nc.vector.quantize_mx(
-                    out=words[:, c0 - lo : c1 - lo].bitcast(FP8X4),
-                    scales=scales[:, c0 - lo : c1 - lo],
-                    in_=g[:, PACK * (c0 - lo) : PACK * (c1 - lo)],
-                )
+        out_acc = {}
+        for m0, n in zip(range(0, T2, P), (3, 4, 5, 7, 0, 1, 2, 6)):
+            out_acc[m0] = banks[n][:, :N].rearrange("p (t m) -> p t m", t=N_TILES)
 
-        def mm(name, b, nt, dst, lo, hi, start=False, stop=False):
-            c0 = b * N + nt * P
-            if name == "dis":
-                lhsT, lhsT_scale = wd_w[:, 2 * c0 : 2 * (c0 + P)].bitcast(FP4X4), wd_sc[:, c0 : c0 + P]
-            else:
-                lhsT, lhsT_scale = wc_w[:, c0 : c0 + P].bitcast(FP8X4), wc_sc[:, c0 : c0 + P]
-            width = hi - lo
-            if width == HALF:
-                cuts = [0, width]
-            elif name == "chg" and width == 3 * P:
-                cuts = [0, 2 * P, width]
-            else:
-                cuts = list(range(0, width + 1, P))
-            for c1, c2 in zip(cuts[:-1], cuts[1:]):
-                words, scales, base = codes[f"{name}{b}", lo + c1]
+        def second_product(name, b, m0, start=False, stop=False):
+            words, scales = codes[name, b, m0]
+            for t in range(N_TILES):
+                c0 = b * N + t * P
+                if name == "dis":
+                    lhsT, lhsT_scale = wd_w[:, 2 * c0 : 2 * (c0 + P)].bitcast(FP4X4), wd_sc[:, c0 : c0 + P]
+                else:
+                    lhsT, lhsT_scale = wc_w[:, c0 : c0 + P].bitcast(FP8X4), wc_sc[:, c0 : c0 + P]
                 nc.tensor.matmul_mx(
-                    out=dst[:, c1:c2],
+                    out=out_acc[m0][:, t, :],
                     lhsT=lhsT,
                     lhsT_scale=lhsT_scale,
-                    rhs=words[:, lo - base + c1 : lo - base + c2].bitcast(FP8X4),
-                    rhs_scale=scales[:, lo - base + c1 : lo - base + c2],
-                    start=start and c1 == 0,
-                    stop=stop and c2 == width,
+                    rhs=words.bitcast(FP8X4),
+                    rhs_scale=scales,
+                    start=(start and t == 0),
+                    stop=(stop and t == N_TILES - 1),
                 )
 
-        quant_w1(0, 0)
-        nc.vector.tensor_copy(v_w[1][:], tab[1][:].indirect(list1[:]))
-        quant_w1(0, 1)
-        nc.vector.tensor_copy(v_w[2][:], tab[2][:].indirect(list1[:]))
-        quant_w1(0, 2)
-
-        turned[0] = keep.tile([P, PACK * T2], BF16, name="turned0", tag="tab0", align_bytes=64)
-        turned[1] = keep.tile([P, 2 * T2], BF16, name="turned1", tag="tab2", align_bytes=64)
-        woven[0] = keep.tile([P, PACK * T2], BF16, name="woven0", tag="tab1", align_bytes=64)
-        pairs = keep.tile([P, PACK * T2], BF16, name="pairs", tag="w1raw0_0", align_bytes=64)
-
-        def sum_block(b, u, n, bank):
-            sum_close(b, u, n, sum_open(b, u, n, bank))
-
-        def pair_back(n, bank):
-            acc = banks[bank]
-            words = turned[1][:].bitcast(F32)
-            for l in range(4):
-                c0 = (4 * n + l) * P
-                nc.tensor.transpose(acc[:, l * P : (l + 1) * P], words[:, c0 : c0 + P], ident[:])
-            nc.scalar.copy(out=pairs[:].bitcast(F32)[:, n * HALF : (n + 1) * HALF], in_=acc[:])
-
-        def add_plane(i, lo, hi):
-            e = i % 2
-            dst = pairs[:].rearrange("p (u m e) -> p u m e", u=2, e=2)[:, 1, lo:hi, e]
-            nc.vector.tensor_tensor(dst, page_of(1, i)[:, lo:hi], inv_sb[1, 1][:, e * T2 + lo : e * T2 + hi], ALU.add)
-
-        def part1(lo, hi, sign, on_scalar, tag):
-            g = keep.tile([P, PACK * (hi - lo)], BF16, name="part1", tag=tag, align_bytes=64)
-            dst = g[:].rearrange("p (m u e) -> p m u e", u=2, e=2)
-            src = pairs[:].rearrange("p (u m e) -> p m u e", u=2, e=2)[:, lo:hi]
-            if on_scalar:
-                nc.scalar.activation(out=dst, in_=src, func=ACT.Relu, scale=sign)
-            else:
-                nc.vector.tensor_scalar(dst, src, sign, 0.0, ALU.mult, ALU.max)
-            return g
-
-        X0, Y0, Z0 = 0, HALF, T2 - P
         for i in range(PACK):
-            scatter(0, i, stage1(0, i))
-        for a in range(KP):
-            quant_w1(1, a)
-        quant_wc()
-        for n in range(3):
-            sum_block(0, 0, n, 4 + n)
-        scatter(1, 0, stage1(1, 0))
-        sum_block(0, 0, 3, 7)
-        for n in range(2):
-            sum_block(0, 1, n, n)
-        scatter(1, 1, stage1(1, 1))
-        for n in range(2, 4):
-            sum_block(0, 1, n, n)
-        scatter(1, 2, stage1(1, 2))
+            product_and_scatter(0, i)
+        for a in range(K_PASSES):
+            quantize_w1(1, a)
+        quantize_wc()
         for n in range(4):
-            turn_back(0, n, n)
-        for lo in (0, HALF):
-            add_plane(2, lo, lo + HALF)
-        dis_a = part(0, X0, Y0, 1.0, True, "w1raw1_0")
-        dis_b = part(0, Y0, T2, 1.0, True, "w1raw2_0")
-        chg0 = part(0, 0, T2, -1.0, False, "w1raw0_512")
-        quant_part("dis0", dis_a, X0, [X0, Y0], tag="tab0")
-        quant_part("chg0", chg0, X0, [X0, T2])
+            sum_quarter(0, 0, n, banks[4 + n])
+        for i in range(2):
+            product_and_scatter(1, i)
         for n in range(4):
-            sum_block(1, 0, n, n)
-        h_last = stage1(1, 3)
+            sum_quarter(0, 1, n, banks[n])
+        product_and_scatter(1, 2)
+        for n in range(4):
+            turn_back_pass0(n, banks[n])
+        add_last_pair(0, 0, T2)
+
+        dis_lo = part("dis", 0, 0, HALF, True, "w1_k1_r0")
+        dis_hi = part("dis", 0, HALF, T2, True, "w1_k2_r0")
+        chg_all = part("chg", 0, 0, T2, False, "w1_k0_r512")
+        quantize_part("dis", 0, dis_lo, 0, [HALF], tag="tab0")
+        quantize_part("chg", 0, chg_all, 0, [T2])
+        for n in range(4):
+            sum_quarter(1, 0, n, banks[n])
+        h_last = keep.tile([P, S], F32, name="h_last", tag="w1_k1_r0", align_bytes=64)
+        first_product(1, 3, h_last)
         for n in range(2):
-            pair_back(n, 4 + n)
-        quant_part("dis0", dis_b, Y0, [Y0, T2], tag="tab2")
+            turn_back_pass1(n, banks[4 + n])
+        quantize_part("dis", 0, dis_hi, HALF, [HALF], tag="tab2")
         scatter(1, 3, h_last)
-        acc = {}
-        for m0, bank in zip(range(0, T2, P), (3, 4, 5, 7, 0, 1, 2, 6)):
-            acc[m0] = banks[bank][:, : NT * P].rearrange("p (t m) -> p t m", t=NT)
-
-        def mm_narrow(name, b, m0, start=False, stop=False):
-            for nt in range(NT):
-                mm(name, b, nt, acc[m0][:, nt, :], m0, m0 + P, start=start and nt == 0, stop=stop and nt == NT - 1)
-
         for m0 in range(0, T2, P):
-            mm_narrow("dis", 0, m0, start=True)
-            mm_narrow("chg", 0, m0)
+            second_product("dis", 0, m0, start=True)
+            second_product("chg", 0, m0)
 
-        def store(m0, width, on_vector):
-            res = ring6.tile([P, NT, width], F32, name="res", bufs=5)
-            for c0 in range(0, width, P):
-                if on_vector[c0 // P]:
-                    nc.vector.tensor_copy(out=res[:, :, c0 : c0 + P], in_=acc[m0 + c0])
-                else:
-                    nc.scalar.copy(out=res[:, :, c0 : c0 + P], in_=acc[m0 + c0])
-            nc.sync.dma_start(out=out[:, m0 : m0 + width].rearrange("(t p) m -> p t m", p=P), in_=res[:])
-
-        Q = 2 * P
-        free_tags = ["w1raw2_256", "w1raw2_512", "w1raw1_512", "wcraw0", "wcraw1", "wc_grouped", "tab1", "w1raw0_512"]
+        spare = ["w1_k2_r256", "w1_k2_r512", "w1_k1_r512", "wc_raw0", "wc_raw1", "wc_cast", "tab1", "w1_k0_r512"]
         parts = {}
 
-        def make(k):
-            parts[k] = (
-                part1(k * Q, (k + 1) * Q, 1.0, k in (0, 1, 2), free_tags[2 * k]),
-                part1(k * Q, (k + 1) * Q, -1.0, False, free_tags[2 * k + 1]),
+        def make_parts(n):
+            lo, hi = n * QUARTER, (n + 1) * QUARTER
+            parts[n] = (
+                part("dis", 1, lo, hi, n < QUARTERS_ON_SCALAR, spare[2 * n]),
+                part("chg", 1, lo, hi, False, spare[2 * n + 1]),
             )
 
-        def finish(k):
-            lo = k * Q
-            last = k == 3
-            quant_part("chg1", parts[k][1], lo, [lo, lo + Q])
-            quant_part("dis1", parts[k][0], lo, [lo, lo + P, lo + Q] if last else [lo, lo + Q])
+        def finish(n):
+            lo = n * QUARTER
+            last = n == 3
+            dis, chg = parts[n]
+            quantize_part("chg", 1, chg, lo, [QUARTER])
+            quantize_part("dis", 1, dis, lo, [P, P] if last else [QUARTER])
             for m0 in (lo, lo + P):
-                mm_narrow("chg", 1, m0)
+                second_product("chg", 1, m0)
             for m0 in (lo, lo + P):
-                mm_narrow("dis", 1, m0, stop=True)
+                second_product("dis", 1, m0, stop=True)
+            result = ring.tile([P, N_TILES, QUARTER], F32, name="result")
             if last:
-                store(lo, P, (True,))
-                store(lo + P, P, (False,))
+                nc.vector.tensor_copy(out=result[:, :, :P], in_=out_acc[lo])
             else:
-                store(lo, Q, (False, False))
+                nc.scalar.copy(out=result[:, :, :P], in_=out_acc[lo])
+            nc.scalar.copy(out=result[:, :, P:], in_=out_acc[lo + P])
+            nc.sync.dma_start(out=out[:, lo : lo + QUARTER].rearrange("(t p) m -> p t m", p=P), in_=result[:])
 
-        add_plane(3, 0, Q)
-        add_plane(3, Q, 2 * Q)
-        make(0)
-        add_plane(3, 2 * Q, T2)
+        add_last_pair(1, 0, QUARTER)
+        add_last_pair(1, QUARTER, HALF)
+        make_parts(0)
+        add_last_pair(1, HALF, T2)
         finish(0)
-        make(1)
-        make(2)
-        finish(1)
-        make(3)
-        finish(2)
-        finish(3)
+        make_parts(1)
+        for n in range(1, 4):
+            if n < 3:
+                make_parts(n + 1)
+            finish(n)

@@ -91,7 +91,7 @@ def tile_list_battery_dispatch_split_kernel(
         load_tab(0)
         load_w1(0, 0)
         for q in range(QUADRANTS):
-            nc.sync.dma_start(
+            nc.scalar.dma_start(
                 out=tab_sc[32 * q : 32 * q + 4 * K_PASSES, :].bitcast(I32),
                 in_=tab_scales[:, 4 * q : 4 * q + 4, :].bitcast(I32),
             )

from contextlib import ExitStack

import concourse.mybir as mybir
from concourse.masks import make_identity

K, T, S, T2, H, N = 1536, 2048, 512, 1024, 1024, 384
FLOPS = 2 * K * H * S + 4 * H * N * T2

F32 = mybir.dt.float32
BF16 = mybir.dt.bfloat16
I32 = mybir.dt.int32
U32 = mybir.dt.uint32
U16 = mybir.dt.uint16
U8 = mybir.dt.uint8
FP8X4 = mybir.dt.float8_e4m3fn_x4
FP4X4 = mybir.dt.float4_e2m1fn_x4
ALU = mybir.AluOpType
ACT = mybir.ActivationFunctionType

P = 128
PACK = 4
PASS = P * PACK
K_PASSES = K // PASS
R_PASSES = H // PASS
N_TILES = N // P
BANK = 512
QUADRANTS = 4
HALF = T2 // 2
QUARTER = T2 // 4
PAGES = 6
QUARTERS_ON_SCALAR = 3


def tile_list_battery_dispatch_split_kernel(
    tc, tab_words, tab_scales, offs, w1, offs2, wgs, inv, wd_words, wd_scales, wc, out
):
    nc = tc.nc
    with ExitStack() as ctx:
        keep = ctx.enter_context(tc.tile_pool(name="keep", bufs=1))
        casts = ctx.enter_context(tc.tile_pool(name="casts", bufs=3))
        ring = ctx.enter_context(tc.tile_pool(name="ring", bufs=4))
        psum = ctx.enter_context(tc.psum_pool(name="psum", bufs=1))
        banks = [psum.tile([P, BANK], F32, name=f"bank{n}") for n in range(8)]

        zones = keep.tile([P, S // 16], U16, name="zones")
        places = keep.tile([P, S // 16], U16, name="places")
        tab_w = [keep.tile([P, T], U32, name=f"tab{a}", align_bytes=64) for a in range(K_PASSES)]
        tab_sc = keep.tile([P, T], U8, name="tab_sc", align_bytes=64)
        wd_sc = keep.tile([P, R_PASSES * N], U8, name="wd_sc", align_bytes=64)
        wd_w = keep.tile([P, R_PASSES * 2 * N], U8, name="wd_w", align_bytes=64)
        wgs_sb = keep.tile([P, S], F32, name="wgs_sb")
        pages = [keep.tile([P, T2], F32, name=f"page{n}") for n in range(PAGES)]

        ident = keep.tile([P, P], F32, name="ident")
        make_identity(nc, ident[:])
        nc.vector.memset(tab_sc[:].bitcast(I32), 0)
        nc.vector.memset(wd_sc[:].bitcast(I32), 0)
        for page in pages:
            nc.vector.memset(page[:], 0.0)

        w1_raw = {}
        inv_sb = {}
        wc_raw = {}

        def load_tab(a):
            nc.sync.dma_start(
                out=tab_w[a][:].bitcast(I32), in_=tab_words[a].rearrange("p t i -> p (t i)").bitcast(I32)
            )

        def load_w1(b, a, pieces=1):
            width = PASS // pieces
            w1_raw[b, a] = []
            for c0 in range(b * PASS, (b + 1) * PASS, width):
                raw = keep.tile([P, PACK, width], F32, name=f"w1_k{a}_r{c0}", align_bytes=64)
                rows = w1[a * PASS : (a + 1) * PASS, c0 : c0 + width]
                nc.sync.dma_start(out=raw[:], in_=rows.rearrange("(p j) c -> p j c", j=PACK))
                w1_raw[b, a].append(raw)

        def load_inv(b, u):
            rows = inv[b * PASS : (b + 1) * PASS, :].rearrange("(p u e) m -> p u (e m)", u=2, e=2)
            inv_sb[b, u] = keep.tile([P, 2 * T2], F32, name=f"inv{b}_{u}")
            nc.sync.dma_start(out=inv_sb[b, u][:], in_=rows[:, u, :])

        def load_wc(b):
            wc_raw[b] = keep.tile([P, PACK, N], F32, name=f"wc_raw{b}", align_bytes=64)
            nc.sync.dma_start(
                out=wc_raw[b][:], in_=wc[b * PASS : (b + 1) * PASS, :].rearrange("(p j) n -> p j n", j=PACK)
            )

        nc.sync.dma_start(zones[:], offs)
        load_tab(0)
        load_w1(0, 0)
        for q in range(QUADRANTS):
            nc.scalar.dma_start(
                out=tab_sc[32 * q : 32 * q + 4 * K_PASSES, :].bitcast(I32),
                in_=tab_scales[:, 4 * q : 4 * q + 4, :].bitcast(I32),
            )
        load_tab(1)
        load_w1(0, 1)
        load_tab(2)
        load_w1(0, 2, pieces=2)
        nc.sync.dma_start(out=wgs_sb[:], in_=wgs)
        nc.sync.dma_start(places[:], offs2)
        for a in range(K_PASSES):
            load_w1(1, a)
        load_inv(0, 0)
        for b in range(R_PASSES):
            load_wc(b)
        load_inv(0, 1)
        nc.sync.dma_start(
            out=wd_w[:].bitcast(I32).rearrange("p (b c) -> p b c", b=R_PASSES),
            in_=wd_words.bitcast(I32).rearrange("b p c -> p b c"),
        )
        for q in range(QUADRANTS):
            nc.sync.dma_start(
                out=wd_sc[32 * q : 32 * q + 4, :].bitcast(I32).rearrange("s (b c) -> s b c", b=R_PASSES),
                in_=wd_scales[:, 4 * q : 4 * q + 4, :].bitcast(I32).rearrange("b s c -> s b c"),
            )
        for u in range(2):
            load_inv(1, u)

        v_sc = keep.tile([P, S], U8, name="v_sc", align_bytes=64)
        v_w = [keep.tile([P, S], U32, name=f"v_w{a}", align_bytes=64) for a in range(K_PASSES)]
        w1_w = {}
        w1_sc = {}

        def quantize(words, scales, values, lo, hi):
            nc.vector.quantize_mx(
                out=words[:, lo:hi].bitcast(FP8X4), scales=scales[:, lo:hi], in_=values[:, PACK * lo : PACK * hi]
            )

        def quantize_w1(b, a):
            cast = casts.tile([P, PACK * PASS], BF16, name="w1_cast", align_bytes=64)
            dst = cast[:].rearrange("p (i m j) -> p m j i", i=PACK, j=PACK)
            src = [raw[:].rearrange("p j (m i) -> p m j i", i=PACK) for raw in w1_raw[b, a]]
            w1_w[b, a] = keep.tile([P, PASS], U32, name=f"w1_w{b}_{a}", align_bytes=64)
            w1_sc[b, a] = keep.tile([P, PASS], U8, name=f"w1_sc{b}_{a}", align_bytes=64)
            if len(src) == 1:
                nc.scalar.activation(out=dst, in_=src[0], func=ACT.Copy)
                quantize(w1_w[b, a], w1_sc[b, a], cast, 0, PASS)
            else:
                nc.scalar.activation(out=dst[:, : P // 2], in_=src[0], func=ACT.Copy)
                nc.vector.tensor_copy(out=dst[:, P // 2 :, :, 0], in_=src[1][:, :, :, 0])
                quantize(w1_w[b, a], w1_sc[b, a], cast, 0, P)
                nc.vector.tensor_copy(out=dst[:, P // 2 :, :, 1:], in_=src[1][:, :, :, 1:])
                quantize(w1_w[b, a], w1_sc[b, a], cast, P, 2 * P)
                quantize(w1_w[b, a], w1_sc[b, a], cast, 2 * P, PASS)

        def first_product(b, i, h):
            bank = banks[PACK * b + i]
            cols = slice(i * P, (i + 1) * P)
            for a in range(K_PASSES):
                nc.tensor.matmul_mx(
                    out=bank[:],
                    lhsT=w1_w[b, a][:, cols].bitcast(FP8X4),
                    lhsT_scale=w1_sc[b, a][:, cols],
                    rhs=v_w[a][:].bitcast(FP8X4),
                    rhs_scale=v_sc[4 * a : P, :],
                    start=(a == 0),
                    stop=(a == K_PASSES - 1),
                )
            nc.scalar.copy(out=h[:], in_=bank[:])

        def page_of(b, i):
            return pages[(PACK * b + i) % PAGES]

        def scatter(b, i, h):
            nc.vector.tensor_tensor(page_of(b, i)[:].indirect(places[:]), h[:], wgs_sb[:], ALU.mult)

        def product_and_scatter(b, i):
            h = ring.tile([P, S], F32, name="h")
            first_product(b, i, h)
            scatter(b, i, h)

        for a in range(K_PASSES):
            nc.vector.tensor_copy(v_w[a][:], tab_w[a][:].indirect(zones[:]))
            if a == 0:
                nc.vector.tensor_copy(v_sc[:], tab_sc[:].indirect(zones[:]))
            quantize_w1(0, a)

        turned = [
            keep.tile([P, PACK * T2], BF16, name="turned0", tag="tab0", align_bytes=64),
            keep.tile([P, 2 * T2], BF16, name="turned1", tag="tab2", align_bytes=64),
        ]
        z0 = keep.tile([P, PACK * T2], BF16, name="z0", tag="tab1", align_bytes=64)
        z1 = keep.tile([P, PACK * T2], BF16, name="z1", tag="w1_k0_r0", align_bytes=64)

        def sum_quarter(b, u, n, bank):
            acc = bank[:].rearrange("q (l e p) -> q l e p", l=2, e=2)
            planes = [(e, inv_sb[b, u][:, e * T2 : (e + 1) * T2]) for e in range(2)]
            planes += [(e, page_of(b, 2 * u + e)[:]) for e in range(2)]
            for step, (e, plane) in enumerate(planes):
                for l in range(2):
                    m0 = n * QUARTER + l * P
                    nc.tensor.matmul(
                        acc[:, l, e, :],
                        lhsT=plane[:, m0 : m0 + P],
                        rhs=ident[:],
                        is_transpose=True,
                        start=(step == 0 and l == 0),
                        stop=(step == len(planes) - 1 and l == 1),
                    )
            c0 = 2 * (u * T2 + n * QUARTER)
            nc.scalar.copy(
                out=turned[b][:, c0 : c0 + 2 * QUARTER].rearrange("q (l p e) -> q l p e", l=2, e=2),
                in_=acc.rearrange("q l e p -> q l p e"),
            )

        def turn_back_pass0(n, bank):
            acc = bank[:].rearrange("p (l u m) -> p l u m", l=2, u=2)
            words = turned[0][:].bitcast(F32)
            for u in range(2):
                for l in range(2):
                    c0 = u * T2 + n * QUARTER + l * P
                    nc.tensor.transpose(acc[:, l, u, :], words[:, c0 : c0 + P], ident[:])
            dst = z0[:].bitcast(F32)[:, 2 * n * QUARTER : 2 * (n + 1) * QUARTER]
            nc.scalar.copy(
                out=dst.rearrange("p (l m u) -> p l m u", l=2, u=2), in_=acc.rearrange("p l u m -> p l m u")
            )

        def turn_back_pass1(n, bank):
            words = turned[1][:].bitcast(F32)
            for c0 in range(0, HALF, P):
                nc.tensor.transpose(bank[:, c0 : c0 + P], words[:, n * HALF + c0 : n * HALF + c0 + P], ident[:])
            nc.scalar.copy(out=z1[:].bitcast(F32)[:, n * HALF : (n + 1) * HALF], in_=bank[:])

        def add_last_pair(e, lo, hi):
            dst = z1[:].rearrange("p (u m e) -> p u m e", u=2, e=2)[:, 1, lo:hi, e]
            nc.vector.tensor_tensor(
                dst, page_of(1, 2 + e)[:, lo:hi], inv_sb[1, 1][:, e * T2 + lo : e * T2 + hi], ALU.add
            )

        SIGN = {"dis": 1.0, "chg": -1.0}
        wc_w = keep.tile([P, R_PASSES * N], U32, name="wc_w", align_bytes=64)
        wc_sc = keep.tile([P, R_PASSES * N], U8, name="wc_sc", align_bytes=64)
        codes = {}

        def quantize_wc():
            cast = keep.tile([P, R_PASSES * PACK * N], BF16, name="wc_cast", align_bytes=64)
            for b in range(R_PASSES):
                nc.scalar.activation(
                    out=cast[:, b * PACK * N : (b + 1) * PACK * N].rearrange("p (c e j) -> p c j e", e=4, j=PACK),
                    in_=wc_raw[b][:].rearrange("p j (c e) -> p c j e", e=4),
                    func=ACT.Copy,
                    scale=-1.0,
                )
            quantize(wc_w, wc_sc, cast, 0, PASS)
            quantize(wc_w, wc_sc, cast, PASS, R_PASSES * N)

        def part(name, b, lo, hi, on_scalar, tag):
            values = keep.tile([P, PACK * (hi - lo)], BF16, name=f"{name}{b}_{lo}", tag=tag, align_bytes=64)
            if b == 0:
                dst, src = values[:], z0[:, PACK * lo : PACK * hi]
            else:
                dst = values[:].rearrange("p (m u e) -> p m u e", u=2, e=2)
                src = z1[:].rearrange("p (u m e) -> p m u e", u=2, e=2)[:, lo:hi]
            if on_scalar:
                nc.scalar.activation(out=dst, in_=src, func=ACT.Relu, scale=SIGN[name])
            else:
                nc.vector.tensor_scalar(dst, src, SIGN[name], 0.0, ALU.mult, ALU.max)
            return values

        def quantize_part(name, b, values, lo, widths, tag=None):
            own = f"{name}{b}_w{lo}"
            words = keep.tile([P, sum(widths)], U32, name=own, tag=tag or own, align_bytes=64)
            scales = keep.tile([P, sum(widths)], U8, name=f"{name}{b}_sc{lo}", align_bytes=64)
            for c0 in range(0, sum(widths), P):
                codes[name, b, lo + c0] = (words[:, c0 : c0 + P], scales[:, c0 : c0 + P])
            for n, width in enumerate(widths):
                quantize(words, scales, values, sum(widths[:n]), sum(widths[:n]) + width)

        out_acc = {}
        for m0, n in zip(range(0, T2, P), (3, 4, 5, 7, 0, 1, 2, 6)):
            out_acc[m0] = banks[n][:, :N].rearrange("p (t m) -> p t m", t=N_TILES)

        def second_product(name, b, m0, start=False, stop=False):
            words, scales = codes[name, b, m0]
            for t in range(N_TILES):
                c0 = b * N + t * P
                if name == "dis":
                    lhsT, lhsT_scale = wd_w[:, 2 * c0 : 2 * (c0 + P)].bitcast(FP4X4), wd_sc[:, c0 : c0 + P]
                else:
                    lhsT, lhsT_scale = wc_w[:, c0 : c0 + P].bitcast(FP8X4), wc_sc[:, c0 : c0 + P]
                nc.tensor.matmul_mx(
                    out=out_acc[m0][:, t, :],
                    lhsT=lhsT,
                    lhsT_scale=lhsT_scale,
                    rhs=words.bitcast(FP8X4),
                    rhs_scale=scales,
                    start=(start and t == 0),
                    stop=(stop and t == N_TILES - 1),
                )

        for i in range(PACK):
            product_and_scatter(0, i)
        for a in range(K_PASSES):
            quantize_w1(1, a)
        quantize_wc()
        for n in range(4):
            sum_quarter(0, 0, n, banks[4 + n])
        for i in range(2):
            product_and_scatter(1, i)
        for n in range(4):
            sum_quarter(0, 1, n, banks[n])
        product_and_scatter(1, 2)
        for n in range(4):
            turn_back_pass0(n, banks[n])
        add_last_pair(0, 0, T2)

        dis_lo = part("dis", 0, 0, HALF, True, "w1_k1_r0")
        dis_hi = part("dis", 0, HALF, T2, True, "w1_k2_r0")
        chg_all = part("chg", 0, 0, T2, False, "w1_k0_r512")
        quantize_part("dis", 0, dis_lo, 0, [HALF], tag="tab0")
        quantize_part("chg", 0, chg_all, 0, [T2])
        for n in range(4):
            sum_quarter(1, 0, n, banks[n])
        h_last = keep.tile([P, S], F32, name="h_last", tag="w1_k1_r0", align_bytes=64)
        first_product(1, 3, h_last)
        for n in range(2):
            turn_back_pass1(n, banks[4 + n])
        quantize_part("dis", 0, dis_hi, HALF, [HALF], tag="tab2")
        scatter(1, 3, h_last)
        for m0 in range(0, T2, P):
            second_product("dis", 0, m0, start=True)
            second_product("chg", 0, m0)

        spare = ["w1_k2_r256", "w1_k2_r512", "w1_k1_r512", "wc_raw0", "wc_raw1", "wc_cast", "tab1", "w1_k0_r512"]
        parts = {}

        def make_parts(n):
            lo, hi = n * QUARTER, (n + 1) * QUARTER
            parts[n] = (
                part("dis", 1, lo, hi, n < QUARTERS_ON_SCALAR, spare[2 * n]),
                part("chg", 1, lo, hi, False, spare[2 * n + 1]),
            )

        def finish(n):
            lo = n * QUARTER
            last = n == 3
            dis, chg = parts[n]
            quantize_part("chg", 1, chg, lo, [QUARTER])
            quantize_part("dis", 1, dis, lo, [P, P] if last else [QUARTER])
            for m0 in (lo, lo + P):
                second_product("chg", 1, m0)
            for m0 in (lo, lo + P):
                second_product("dis", 1, m0, stop=True)
            result = ring.tile([P, N_TILES, QUARTER], F32, name="result")
            if last:
                nc.vector.tensor_copy(out=result[:, :, :P], in_=out_acc[lo])
            else:
                nc.scalar.copy(out=result[:, :, :P], in_=out_acc[lo])
            nc.scalar.copy(out=result[:, :, P:], in_=out_acc[lo + P])
            nc.sync.dma_start(out=out[:, lo : lo + QUARTER].rearrange("(t p) m -> p t m", p=P), in_=result[:])

        add_last_pair(1, 0, QUARTER)
        add_last_pair(1, QUARTER, HALF)
        make_parts(0)
        add_last_pair(1, HALF, T2)
        finish(0)
        make_parts(1)
        for n in range(1, 4):
            if n < 3:
                make_parts(n + 1)
            finish(n)
